import numpy as np
import ml_dtypes


def mxq(x, axis, fmt="e4m3"):
    dtype, down = {"e4m3": (ml_dtypes.float8_e4m3fn, 7), "e5m2": (ml_dtypes.float8_e5m2, 14)}[fmt]
    v = np.moveaxis(np.asarray(x, np.float32).astype(ml_dtypes.bfloat16).astype(np.float64), axis, -1)
    blocks = v.reshape(v.shape[:-1] + (-1, 32))
    amax = np.abs(blocks).max(-1, keepdims=True)
    byte = np.maximum(np.where(amax > 0, np.frexp(amax)[1] - 1 + 127, 0) - down, 1)
    scale = np.exp2(byte - 127.0)
    codes = (blocks / scale).astype(np.float32).astype(dtype).astype(np.float64)
    return np.moveaxis((codes * scale).reshape(v.shape), -1, axis)


WIDE = False


def mx_kscale(k):
    if not WIDE:
        return np.ones(k)
    levels = np.array([10, -10, 5, -5, 0])
    if k % 512:
        return np.exp2(np.random.permutation(np.resize(levels, k // 32))).repeat(32)
    a = np.empty((k // 512, 16))
    for p in range(k // 512):
        a[p, :8] = np.random.permutation(np.resize(levels, 8))
        for g in range(8):
            far = levels[np.abs(levels - a[p, g]) >= 10]
            a[p, g + 8] = far[np.random.randint(len(far))]
    return np.exp2(a.ravel()).repeat(32)


def f64(x):
    return np.asarray(x).astype(np.float64)


def striped(idx):
    return np.tile(idx.reshape(-1, 16).T, (8, 1)).astype(np.uint16)


def unstriped(offs):
    return offs[:16].T.reshape(-1).astype(np.int64)


def striped8(idx):
    return np.concatenate([x.reshape(-1, 16).T for x in idx]).astype(np.uint16)


def runs(offs, k):
    lists = np.stack([offs[16 * r : 16 * r + 16].T.reshape(-1) for r in range(8)]).astype(np.int64)
    return lists[np.arange(k) % 512 // 64]


def pack_weight(w):
    k, n = w.shape
    w = f64(np.asarray(w, np.float32).astype(ml_dtypes.bfloat16)).reshape(k // 32, 32, n)
    amax = np.abs(w).max(1)
    byte = np.clip(np.where(amax > 0, np.frexp(amax)[1] - 1 + 127 - 7, 1), 1, 254)
    scaled = (w * np.exp2(127.0 - byte)[:, None, :]).reshape(k, n).astype(np.float32)
    words = np.ascontiguousarray(scaled.reshape(k // 512, 128, 4, n).transpose(0, 1, 3, 2)).astype(ml_dtypes.float8_e4m3fn).view(np.uint8)
    return words, np.ascontiguousarray(byte.astype(np.uint8).reshape(k // 512, 16, n))


def unpack_weight(words, scales):
    g, p, n, _ = words.shape
    vals = np.ascontiguousarray(words).view(ml_dtypes.float8_e4m3fn).astype(np.float64) * np.repeat(np.exp2(scales.astype(np.float64) - 127.0), 8, axis=1)[..., None]
    return vals.transpose(0, 1, 3, 2).reshape(g * 512, n)


K, T, S, V, H = 512, 2048, 512, 512, 512


def setup_inputs():
    n = np.random.standard_normal
    s = mx_kscale(K)[:, None]
    u = mx_kscale(S)
    packed_xT = pack_weight(n((K, T)) * s)
    return {
        "x_words": packed_xT[0],
        "x_scales": packed_xT[1],
        "w1": (n((K, H)) / np.sqrt(K) / s).astype(np.float32),
        "w2": (n((K, H)) / np.sqrt(K) / s).astype(np.float32),
        "tau": np.random.uniform(0.3, 0.9, (H, 1)).astype(np.float32),
        "tau2": np.random.uniform(0.3, 0.9, (H, 1)).astype(np.float32),
        "tau3": np.random.uniform(0.3, 0.9, (H, 1)).astype(np.float32),
        "ga": (np.random.uniform(0.5, 1.5, (H, 1)) * u[:, None]).astype(np.float32),
        "gb": (np.random.uniform(0.5, 1.5, (H, 1)) / u[:, None]).astype(np.float32),
        "tau4": np.random.uniform(0.3, 0.9, (S, 1)).astype(np.float32),
        "offs": striped8(np.random.randint(0, T, (8, S))),
        "two": striped(np.random.permutation(T)[:V]),
        "n1": striped8(np.stack([np.random.permutation(S) for _ in range(8)])),
        "n2": striped8(np.stack([np.random.permutation(S) for _ in range(8)])),
        "n3": striped8(np.stack([np.random.permutation(V) for _ in range(8)])),
        "n4": striped8(np.stack([np.random.permutation(V) for _ in range(8)])),
        "n5": striped8(np.stack([np.random.permutation(V) for _ in range(8)])),
    }


def reference(x_words, x_scales, w1, w2, tau, tau2, tau3, ga, gb, tau4, offs, two, n1, n2, n3, n4, n5):
    xq = unpack_weight(x_words, x_scales)[np.arange(K)[:, None], runs(offs, K)]
    a = mxq(f64(w1), 0, "e4m3").T @ xq
    top = a.max(axis=1, keepdims=True)
    ea = np.exp(f64(tau) * (a[np.arange(H)[:, None], runs(n1, H)] - top))
    low = a.min(axis=1, keepdims=True)
    ea2 = np.exp(f64(tau2) * (low - (a[np.arange(H)[:, None], runs(n2, H)])))
    z = f64(ga) * (1.5 * (a * (ea + ea2)))
    x_two = unpack_weight(x_words, x_scales)[:, unstriped(two)]
    b = mxq(f64(w2), 0, "e4m3").T @ x_two
    top2 = b.max(axis=1, keepdims=True)
    own = np.exp(f64(tau3) * (b - top2))
    ea3 = np.exp(f64(tau3) * (b[np.arange(H)[:, None], runs(n3, H)] - top2))
    z2 = f64(gb) * ((2.0 * (b * own)) / (own + ea3 + 0.25))
    s = 0.0625 * ((mxq(z, 0, "e4m3").T @ mxq(z2, 0, "e4m3")))
    sq = (s) ** 2
    ea4 = np.exp(-1.0 * (f64(tau4) * (sq[np.arange(S)[:, None], runs(n4, S)])))
    return s * ea4 - (0.5 * (s[np.arange(S)[:, None], runs(n5, S)]))

@@ -1,0 +1,264 @@
+from contextlib import ExitStack
+
+import concourse.mybir as mybir
+
+K, T, S, V, H = 512, 2048, 512, 512, 512
+FLOPS = 2 * K * H * S + 2 * K * H * V + 2 * H * S * V
+
+F32 = mybir.dt.float32
+BF16 = mybir.dt.bfloat16
+I32 = mybir.dt.int32
+U32 = mybir.dt.uint32
+U16 = mybir.dt.uint16
+U8 = mybir.dt.uint8
+FP8X4 = mybir.dt.float8_e4m3fn_x4
+ALU = mybir.AluOpType
+ACT = mybir.ActivationFunctionType
+AXIS_X = mybir.AxisListType.X
+
+P = 128
+PACK = 4
+N = 512
+HALF = N // 2
+WINDOW = 2 * N
+SCALE_ROWS = 16
+
+
+def tile_picked_hkqedfeshega_none_p_kernel(
+    tc, x_words, x_scales, w1, w2, tau, tau2, tau3, ga, gb, tau4, offs, two, n1, n2, n3, n4, n5, out
+):
+    nc = tc.nc
+    tiles = range(PACK)
+
+    with ExitStack() as ctx:
+        lists = ctx.enter_context(tc.tile_pool(name="lists", bufs=1))
+        keep = ctx.enter_context(tc.tile_pool(name="keep", bufs=1))
+        psum = ctx.enter_context(tc.psum_pool(name="psum", bufs=1))
+
+        def load_list(name, src):
+            dst = lists.tile([P, N // 16], U16, name=name)
+            nc.sync.dma_start(dst[:], src)
+            return dst
+
+        def load_column(name, src):
+            dst = keep.tile([P, PACK], F32, name=name)
+            nc.gpsimd.dma_start(dst[:], src.rearrange("(p t) o -> p (t o)", t=PACK))
+            return dst
+
+        offs_sb = load_list("offs_sb", offs)
+        table_scales = keep.tile([P, T], U8, name="table_scales")
+        nc.scalar.dma_start(
+            table_scales[:].bitcast(I32),
+            x_scales[0].bitcast(I32).unsqueeze(1).broadcast_to([SCALE_ROWS, P // SCALE_ROWS, T // 4]),
+        )
+        two_sb = load_list("two_sb", two)
+        table_words = keep.tile([P, T], I32, name="table_words")
+        nc.sync.dma_start(table_words[:], x_words[0].rearrange("p n t -> p (n t)").bitcast(I32))
+        w_raw = [keep.tile([P, PACK, HALF], F32, name="w_raw%d" % h) for h in range(2)]
+
+        def load_weight(w):
+            rows = w.rearrange("(p j) c -> p j c", j=PACK)
+            for h in range(2):
+                nc.sync.dma_start(w_raw[h][:], rows[:, :, h * HALF : (h + 1) * HALF])
+
+        load_weight(w1)
+
+        tau_sb = load_column("tau_sb", tau)
+        tau2_sb = load_column("tau2_sb", tau2)
+        win_a = [keep.tile([P, WINDOW], F32, name="win_a%d" % t) for t in tiles]
+        win_b = [keep.tile([P, WINDOW], F32, name="win_b%d" % t) for t in tiles]
+        nc.gpsimd.memset(win_a[0][:, N:], 0.0)
+        rate_a = keep.tile([P, PACK, 2], F32, name="rate_a")
+        neg_tau2 = keep.tile([P, PACK], F32, name="neg_tau2")
+
+        def scaled(dst, src, factor):
+            nc.gpsimd.tensor_scalar(dst, src, factor, 0.0, ALU.mult, ALU.add)
+
+        scaled(rate_a[:, :, 0], tau_sb[:], -1.0)
+        scaled(rate_a[:, :, 1], tau2_sb[:], 1.0)
+        scaled(neg_tau2[:], tau2_sb[:], -1.0)
+        for t in tiles[1:]:
+            nc.gpsimd.memset(win_a[t][:, N:], 0.0)
+        ga_sb = load_column("ga_sb", ga)
+        tau3_sb = load_column("tau3_sb", tau3)
+        gb_sb = load_column("gb_sb", gb)
+        tau4_sb = load_column("tau4_sb", tau4)
+        gain_a = keep.tile([P, PACK], F32, name="gain_a")
+        gain_b = keep.tile([P, PACK], F32, name="gain_b")
+        neg_tau4 = keep.tile([P, PACK], F32, name="neg_tau4")
+        quarter = keep.tile([P, 1], F32, name="quarter")
+        scaled(gain_a[:], ga_sb[:], 1.5)
+        scaled(gain_b[:], gb_sb[:], 2.0)
+        scaled(neg_tau4[:], tau4_sb[:], -1.0)
+        nc.gpsimd.memset(quarter[:], 0.25)
+
+        picked_scales = keep.tile([P, 2 * N], U8, name="picked_scales")
+        x_planes = keep.tile([P, 2 * N], U8, name="x_planes", align_bytes=64)
+        nc.vector.memset(x_planes[:].bitcast(I32), 0)
+        nc.vector.tensor_copy(picked_scales[:, :N], table_scales[:].indirect(offs_sb[:]))
+        nc.vector.tensor_copy(picked_scales[:, N:], table_scales[:].indirect(two_sb[:]))
+        for j in range(4):
+            nc.sync.dma_start(
+                x_planes[:].bitcast(I32)[j:P:32, :], picked_scales[:].bitcast(I32)[8 * j : P : 32, :]
+            )
+        n1_sb = load_list("n1_sb", n1)
+        n2_sb = load_list("n2_sb", n2)
+        n3_sb = load_list("n3_sb", n3)
+        n4_sb = load_list("n4_sb", n4)
+        n5_sb = load_list("n5_sb", n5)
+        xa_words = keep.tile([P, N], U32, name="xa_words", align_bytes=64)
+        xb_words = keep.tile([P, N], U32, name="xb_words", align_bytes=64)
+        nc.vector.tensor_copy(xa_words[:], table_words[:].bitcast(U32).indirect(offs_sb[:]))
+        nc.vector.tensor_copy(xb_words[:], table_words[:].bitcast(U32).indirect(two_sb[:]))
+
+        def dealt(grouped, m0, m1):
+            return grouped[:].rearrange("p (t m j) -> p m j t", t=PACK, j=PACK)[:, m0:m1]
+
+        def raw(h, m0, m1):
+            return w_raw[h][:].rearrange("p j (m t) -> p m j t", t=PACK)[:, m0:m1]
+
+        w1_bf = keep.tile([P, PACK * N], BF16, name="w1_bf", align_bytes=64)
+        nc.scalar.activation(dealt(w1_bf, 0, 64), raw(0, 0, 64), ACT.Copy)
+        nc.scalar.activation(dealt(w1_bf, 64, 88), raw(1, 0, 24), ACT.Copy)
+        nc.vector.tensor_copy(dealt(w1_bf, 88, 128), raw(1, 24, 64))
+        w1_codes = keep.tile([P, N], U32, name="w1_codes", align_bytes=64)
+        w1_plane = keep.tile([P, N], U8, name="w1_plane", align_bytes=64)
+
+        load_weight(w2)
+
+        bank_a = [psum.tile([P, N], F32, name="bank_a%d" % t) for t in tiles]
+        bank_b = [psum.tile([P, N], F32, name="bank_b%d" % t) for t in tiles]
+
+        def product(bank, lhs_codes, lhs_plane, t, rhs_codes, rhs_plane):
+            cols = slice(P * t, P * (t + 1))
+            nc.tensor.matmul_mx(
+                out=bank,
+                lhsT=lhs_codes[:, cols].bitcast(FP8X4),
+                lhsT_scale=lhs_plane[:, cols],
+                rhs=rhs_codes.bitcast(FP8X4),
+                rhs_scale=rhs_plane,
+                start=True,
+                stop=True,
+            )
+
+        for t in tiles:
+            cols = slice(P * t, P * (t + 1))
+            nc.vector.quantize_mx(
+                out=w1_codes[:, cols].bitcast(FP8X4), scales=w1_plane[:, cols], in_=w1_bf[:, N * t : N * (t + 1)]
+            )
+            product(bank_a[t][:], w1_codes, w1_plane, t, xa_words[:], x_planes[:, :N])
+
+        ends_a = keep.tile([P, PACK, 2], F32, name="ends_a")
+        bias_a = keep.tile([P, PACK, 2], F32, name="bias_a")
+        ea2 = keep.tile([P, PACK, N], F32, name="ea2")
+        for t in tiles:
+            nc.vector.tensor_scalar(
+                win_a[t][:, :N], bank_a[t][:], 1.0, None, ALU.mult, ALU.max, accum_out=ends_a[:, t, 0:1]
+            )
+            if t == 0:
+                nc.vector.tensor_tensor(bias_a[:, t, 0:1], ends_a[:, t, 0:1], rate_a[:, t, 0:1], ALU.mult)
+            nc.vector.tensor_reduce(ends_a[:, t, 1:2], bank_a[t][:], AXIS_X, ALU.min)
+            if t == 0:
+                nc.vector.tensor_tensor(bias_a[:, t, 1:2], ends_a[:, t, 1:2], rate_a[:, t, 1:2], ALU.mult)
+            else:
+                nc.vector.tensor_tensor(bias_a[:, t, :], ends_a[:, t, :], rate_a[:, t, :], ALU.mult)
+            nc.scalar.activation(
+                win_b[t][:, N:], win_a[t][:].indirect(n1_sb[:]), ACT.Exp,
+                bias=bias_a[:, t, 0:1], scale=tau_sb[:, t : t + 1],
+            )
+            nc.scalar.activation(
+                ea2[:, t, :], win_a[t][:].indirect(n2_sb[:]), ACT.Exp,
+                bias=bias_a[:, t, 1:2], scale=neg_tau2[:, t : t + 1],
+            )
+
+        w2_bf = keep.tile([P, PACK * N], BF16, name="w2_bf", align_bytes=64)
+        for h in range(2):
+            nc.vector.tensor_copy(dealt(w2_bf, 64 * h, 64 * (h + 1)), raw(h, 0, 64))
+        w2_codes = keep.tile([P, N], U32, name="w2_codes", align_bytes=64)
+        w2_plane = keep.tile([P, N], U8, name="w2_plane", align_bytes=64)
+        nc.vector.quantize_mx(out=w2_codes[:].bitcast(FP8X4), scales=w2_plane[:], in_=w2_bf[:])
+        top_b = keep.tile([P, PACK], F32, name="top_b")
+        bias_b = keep.tile([P, PACK], F32, name="bias_b")
+        for t in tiles:
+            product(bank_b[t][:], w2_codes, w2_plane, t, xb_words[:], x_planes[:, N:])
+            nc.vector.tensor_scalar(
+                win_b[t][:, :N], bank_b[t][:], 1.0, None, ALU.mult, ALU.max, accum_out=top_b[:, t : t + 1]
+            )
+        nc.vector.scalar_tensor_tensor(bias_b[:], top_b[:], -1.0, tau3_sb[:], ALU.mult, ALU.mult)
+        ea3 = keep.tile([P, PACK, N], F32, name="ea3")
+        for t in tiles:
+            nc.scalar.activation(
+                ea3[:, t, :], win_b[t][:].indirect(n3_sb[:]), ACT.Exp,
+                bias=bias_b[:, t : t + 1], scale=tau3_sb[:, t : t + 1],
+            )
+
+        ea_sum = keep.tile([P, PACK, N], F32, name="ea_sum")
+        z_bf = keep.tile([P, PACK, N], BF16, name="z_bf")
+        for t in tiles:
+            nc.vector.tensor_tensor(ea_sum[:, t, :], win_b[t][:, N:], ea2[:, t, :], ALU.add)
+        for t in tiles:
+            nc.vector.scalar_tensor_tensor(
+                z_bf[:, t, :], bank_a[t][:], gain_a[:, t : t + 1], ea_sum[:, t, :], ALU.mult, ALU.mult
+            )
+        z_grouped = keep.tile([P, PACK * N], BF16, name="z_grouped", align_bytes=64)
+        nc.vector.tensor_copy(
+            z_grouped[:].rearrange("p (u m t) -> p m t u", u=PACK, t=PACK),
+            z_bf[:].rearrange("p t (m u) -> p m t u", u=PACK),
+        )
+        z_codes = keep.tile([P, N], U32, name="z_codes", align_bytes=64)
+        z_plane = keep.tile([P, N], U8, name="z_plane", align_bytes=64)
+
+        rest = ea2
+        logit = keep.tile([P, PACK, N], F32, name="logit")
+        for t in tiles:
+            nc.scalar.activation(rest[:, t, :], ea3[:, t, :], ACT.Ln, bias=quarter[:])
+            nc.vector.scalar_tensor_tensor(
+                logit[:, t, :], bank_b[t][:], tau3_sb[:, t : t + 1], rest[:, t, :], ALU.mult, ALU.subtract
+            )
+        nc.vector.quantize_mx(out=z_codes[:].bitcast(FP8X4), scales=z_plane[:], in_=z_grouped[:])
+        share = ea3
+        z2_bf = keep.tile([P, PACK, N], BF16, name="z2_bf")
+        z2_grouped = keep.tile([P, PACK * N], BF16, name="z2_grouped", align_bytes=64)
+        z2_codes = keep.tile([P, N], U32, name="z2_codes", align_bytes=64)
+        z2_plane = keep.tile([P, N], U8, name="z2_plane", align_bytes=64)
+        bank_s = bank_a
+        for h in range(2):
+            cols = slice(HALF * h, HALF * (h + 1))
+            wide = slice(PACK * HALF * h, PACK * HALF * (h + 1))
+            for t in tiles:
+                nc.scalar.activation(share[:, t, cols], logit[:, t, cols], ACT.Sigmoid, bias=bias_b[:, t : t + 1])
+                nc.vector.scalar_tensor_tensor(
+                    z2_bf[:, t, cols], bank_b[t][:, cols], gain_b[:, t : t + 1], share[:, t, cols], ALU.mult, ALU.mult
+                )
+            nc.vector.tensor_copy(
+                z2_grouped[:, wide].rearrange("p (c i t) -> p c t i", i=4, t=PACK),
+                z2_bf[:, :, cols].rearrange("p t (c i) -> p c t i", i=4),
+            )
+            nc.vector.quantize_mx(out=z2_codes[:, cols].bitcast(FP8X4), scales=z2_plane[:, cols], in_=z2_grouped[:, wide])
+            for t in tiles:
+                product(bank_s[t][:, cols], z_codes, z_plane, t, z2_codes[:, cols], z2_plane[:, cols])
+
+        out_rows = out.rearrange("(p t) v -> p t v", t=PACK)
+        ea4 = logit
+        kept = ea_sum
+        win_sq, win_half = win_a, win_b
+        for t in tiles:
+            result = keep.tile([P, N], F32, name="result%d" % t)
+            if t == 0:
+                nc.scalar.activation(win_sq[t][:, :N], bank_s[t][:], ACT.Square, scale=0.0625)
+            nc.vector.tensor_scalar(win_half[t][:, :N], bank_s[t][:], -0.03125, None, ALU.mult)
+            if t > 0:
+                nc.scalar.activation(win_sq[t][:, :N], bank_s[t][:], ACT.Square, scale=0.0625)
+            pieces = [(0, N)] if t < PACK - 1 else [(0, HALF), (HALF, N)]
+            for c0, c1 in pieces:
+                entries = slice(c0 // 16, c1 // 16)
+                nc.scalar.activation(
+                    ea4[:, t, c0:c1], win_sq[t][:].indirect(n4_sb[:, entries]), ACT.Exp, scale=neg_tau4[:, t : t + 1]
+                )
+                nc.vector.scalar_tensor_tensor(
+                    kept[:, t, c0:c1], bank_s[t][:, c0:c1], 0.0625, ea4[:, t, c0:c1], ALU.mult, ALU.mult
+                )
+                nc.vector.tensor_tensor(
+                    result[:, c0:c1], win_half[t][:].indirect(n5_sb[:, entries]), kept[:, t, c0:c1], ALU.add
+                )
+                nc.sync.dma_start(out_rows[:, t, c0:c1], result[:, c0:c1])

@@ -46,7 +46,7 @@ def tile_picked_hkqedfeshega_none_p_kernel(
             return dst
 
         offs_sb = load_list("offs_sb", offs)
-        table_scales = keep.tile([P, T], U8, name="table_scales")
+        table_scales = keep.tile([P, T], U8, name="table_scales", tag="staging")
         nc.scalar.dma_start(
             table_scales[:].bitcast(I32),
             x_scales[0].bitcast(I32).unsqueeze(1).broadcast_to([SCALE_ROWS, P // SCALE_ROWS, T // 4]),
@@ -54,6 +54,8 @@ def tile_picked_hkqedfeshega_none_p_kernel(
         two_sb = load_list("two_sb", two)
         table_words = keep.tile([P, T], I32, name="table_words")
         nc.sync.dma_start(table_words[:], x_words[0].rearrange("p n t -> p (n t)").bitcast(I32))
+        n1_sb = load_list("n1_sb", n1)
+        n2_sb = load_list("n2_sb", n2)
         w_raw = [keep.tile([P, PACK, HALF], F32, name="w_raw%d" % h) for h in range(2)]
 
         def load_weight(w):
@@ -101,8 +103,8 @@ def tile_picked_hkqedfeshega_none_p_kernel(
             nc.sync.dma_start(
                 x_planes[:].bitcast(I32)[j:P:32, :], picked_scales[:].bitcast(I32)[8 * j : P : 32, :]
             )
-        n1_sb = load_list("n1_sb", n1)
-        n2_sb = load_list("n2_sb", n2)
+        w2_raw = keep.tile([P, PACK, N], F32, name="w2_raw", tag="staging")
+        nc.sync.dma_start(w2_raw[:], w2.rearrange("(p j) c -> p j c", j=PACK))
         n3_sb = load_list("n3_sb", n3)
         n4_sb = load_list("n4_sb", n4)
         n5_sb = load_list("n5_sb", n5)
@@ -123,8 +125,6 @@ def tile_picked_hkqedfeshega_none_p_kernel(
         nc.vector.tensor_copy(dealt(w1_bf, 88, 128), raw(1, 24, 64))
         w1_codes = keep.tile([P, N], U32, name="w1_codes", align_bytes=64)
         w1_plane = keep.tile([P, N], U8, name="w1_plane", align_bytes=64)
-
-        load_weight(w2)
 
         bank_a = [psum.tile([P, N], F32, name="bank_a%d" % t) for t in tiles]
         bank_b = [psum.tile([P, N], F32, name="bank_b%d" % t) for t in tiles]
@@ -171,9 +171,8 @@ def tile_picked_hkqedfeshega_none_p_kernel(
                 bias=bias_a[:, t, 1:2], scale=neg_tau2[:, t : t + 1],
             )
 
-        w2_bf = keep.tile([P, PACK * N], BF16, name="w2_bf", align_bytes=64)
-        for h in range(2):
-            nc.vector.tensor_copy(dealt(w2_bf, 64 * h, 64 * (h + 1)), raw(h, 0, 64))
+        w2_bf = keep.tile([P, PACK * N], BF16, name="w2_bf", tag="rounded", align_bytes=64)
+        nc.vector.tensor_copy(dealt(w2_bf, 0, P), w2_raw[:].rearrange("p j (m t) -> p m j t", t=PACK))
         w2_codes = keep.tile([P, N], U32, name="w2_codes", align_bytes=64)
         w2_plane = keep.tile([P, N], U8, name="w2_plane", align_bytes=64)
         nc.vector.quantize_mx(out=w2_codes[:].bitcast(FP8X4), scales=w2_plane[:], in_=w2_bf[:])
@@ -184,7 +183,9 @@ def tile_picked_hkqedfeshega_none_p_kernel(
             nc.vector.tensor_scalar(
                 win_b[t][:, :N], bank_b[t][:], 1.0, None, ALU.mult, ALU.max, accum_out=top_b[:, t : t + 1]
             )
-        nc.vector.scalar_tensor_tensor(bias_b[:], top_b[:], -1.0, tau3_sb[:], ALU.mult, ALU.mult)
+            nc.vector.tensor_scalar(
+                bias_b[:, t : t + 1], top_b[:, t : t + 1], tau3_sb[:, t : t + 1], -1.0, ALU.mult, ALU.mult
+            )
         ea3 = keep.tile([P, PACK, N], F32, name="ea3")
         for t in tiles:
             nc.scalar.activation(
@@ -193,9 +194,9 @@ def tile_picked_hkqedfeshega_none_p_kernel(
             )
 
         ea_sum = keep.tile([P, PACK, N], F32, name="ea_sum")
-        z_bf = keep.tile([P, PACK, N], BF16, name="z_bf")
+        z_bf = keep.tile([P, PACK, N], BF16, name="z_bf", tag="rounded", align_bytes=64)
         for t in tiles:
-            nc.vector.tensor_tensor(ea_sum[:, t, :], win_b[t][:, N:], ea2[:, t, :], ALU.add)
+            nc.gpsimd.tensor_tensor(ea_sum[:, t, :], win_b[t][:, N:], ea2[:, t, :], ALU.add)
         for t in tiles:
             nc.vector.scalar_tensor_tensor(
                 z_bf[:, t, :], bank_a[t][:], gain_a[:, t : t + 1], ea_sum[:, t, :], ALU.mult, ALU.mult
@@ -208,31 +209,34 @@ def tile_picked_hkqedfeshega_none_p_kernel(
         z_codes = keep.tile([P, N], U32, name="z_codes", align_bytes=64)
         z_plane = keep.tile([P, N], U8, name="z_plane", align_bytes=64)
 
-        rest = ea2
-        logit = keep.tile([P, PACK, N], F32, name="logit")
+        b_gain = keep.tile([P, PACK, N], F32, name="b_gain")
         for t in tiles:
-            nc.scalar.activation(rest[:, t, :], ea3[:, t, :], ACT.Ln, bias=quarter[:])
-            nc.vector.scalar_tensor_tensor(
-                logit[:, t, :], bank_b[t][:], tau3_sb[:, t : t + 1], rest[:, t, :], ALU.mult, ALU.subtract
-            )
+            nc.gpsimd.tensor_scalar(b_gain[:, t, :], win_b[t][:, :N], gain_b[:, t : t + 1], 0.0, ALU.mult, ALU.add)
+        rest = keep.tile([P, PACK, N], F32, name="rest")
+        logit = keep.tile([P, PACK, N], F32, name="logit")
+        for h in range(2):
+            cols = slice(HALF * h, HALF * (h + 1))
+            nc.scalar.activation(rest[:, :, cols], ea3[:, :, cols], ACT.Ln, bias=quarter[:])
+            for t in tiles:
+                nc.vector.scalar_tensor_tensor(
+                    logit[:, t, cols], bank_b[t][:, cols], tau3_sb[:, t : t + 1], rest[:, t, cols], ALU.mult, ALU.subtract
+                )
         nc.vector.quantize_mx(out=z_codes[:].bitcast(FP8X4), scales=z_plane[:], in_=z_grouped[:])
         share = ea3
-        z2_bf = keep.tile([P, PACK, N], BF16, name="z2_bf")
         z2_grouped = keep.tile([P, PACK * N], BF16, name="z2_grouped", align_bytes=64)
         z2_codes = keep.tile([P, N], U32, name="z2_codes", align_bytes=64)
         z2_plane = keep.tile([P, N], U8, name="z2_plane", align_bytes=64)
         bank_s = bank_a
-        for h in range(2):
-            cols = slice(HALF * h, HALF * (h + 1))
-            wide = slice(PACK * HALF * h, PACK * HALF * (h + 1))
+        for c in range(N // P):
+            cols = slice(P * c, P * (c + 1))
+            wide = slice(PACK * P * c, PACK * P * (c + 1))
             for t in tiles:
                 nc.scalar.activation(share[:, t, cols], logit[:, t, cols], ACT.Sigmoid, bias=bias_b[:, t : t + 1])
-                nc.vector.scalar_tensor_tensor(
-                    z2_bf[:, t, cols], bank_b[t][:, cols], gain_b[:, t : t + 1], share[:, t, cols], ALU.mult, ALU.mult
-                )
-            nc.vector.tensor_copy(
-                z2_grouped[:, wide].rearrange("p (c i t) -> p c t i", i=4, t=PACK),
-                z2_bf[:, :, cols].rearrange("p t (c i) -> p c t i", i=4),
+            nc.vector.tensor_tensor(
+                z2_grouped[:, wide].rearrange("p (c i t) -> p c t i", i=2, t=PACK),
+                b_gain[:, :, cols].rearrange("p t (c i) -> p c t i", i=2),
+                share[:, :, cols].rearrange("p t (c i) -> p c t i", i=2),
+                ALU.mult,
             )
             nc.vector.quantize_mx(out=z2_codes[:, cols].bitcast(FP8X4), scales=z2_plane[:, cols], in_=z2_grouped[:, wide])
             for t in tiles:
@@ -246,7 +250,10 @@ def tile_picked_hkqedfeshega_none_p_kernel(
             result = keep.tile([P, N], F32, name="result%d" % t)
             if t == 0:
                 nc.scalar.activation(win_sq[t][:, :N], bank_s[t][:], ACT.Square, scale=0.0625)
-            nc.vector.tensor_scalar(win_half[t][:, :N], bank_s[t][:], -0.03125, None, ALU.mult)
+            if t < PACK - 1:
+                nc.vector.tensor_scalar(win_half[t][:, :N], bank_s[t][:], -0.03125, None, ALU.mult)
+            else:
+                nc.scalar.activation(win_half[t][:, :N], bank_s[t][:], ACT.Copy, scale=-0.03125)
             if t > 0:
                 nc.scalar.activation(win_sq[t][:, :N], bank_s[t][:], ACT.Square, scale=0.0625)
             pieces = [(0, N)] if t < PACK - 1 else [(0, HALF), (HALF, N)]

@@ -242,6 +242,9 @@ def tile_picked_hkqedfeshega_none_p_kernel(
             for t in tiles:
                 product(bank_s[t][:, cols], z_codes, z_plane, t, z2_codes[:, cols], z2_plane[:, cols])
 
+        table_warm = keep.tile([P, 1], F32, name="table_warm")
+        nc.scalar.activation(table_warm[:], share[:, 0, N - 1 : N], ACT.Exp)
+
         out_rows = out.rearrange("(p t) v -> p t v", t=PACK)
         ea4 = logit
         kept = ea_sum

@@ -108,10 +108,8 @@ def tile_picked_hkqedfeshega_none_p_kernel(
         n3_sb = load_list("n3_sb", n3)
         n4_sb = load_list("n4_sb", n4)
         n5_sb = load_list("n5_sb", n5)
-        xa_words = keep.tile([P, N], U32, name="xa_words", align_bytes=64)
-        xb_words = keep.tile([P, N], U32, name="xb_words", align_bytes=64)
+        xa_words = keep.tile([P, N], U32, name="xa_words", tag="picked_words", align_bytes=64)
         nc.vector.tensor_copy(xa_words[:], table_words[:].bitcast(U32).indirect(offs_sb[:]))
-        nc.vector.tensor_copy(xb_words[:], table_words[:].bitcast(U32).indirect(two_sb[:]))
 
         def dealt(grouped, m0, m1):
             return grouped[:].rearrange("p (t m j) -> p m j t", t=PACK, j=PACK)[:, m0:m1]
@@ -171,15 +169,21 @@ def tile_picked_hkqedfeshega_none_p_kernel(
                 bias=bias_a[:, t, 1:2], scale=neg_tau2[:, t : t + 1],
             )
 
+        xb_words = keep.tile([P, N], U32, name="xb_words", tag="picked_words", align_bytes=64)
+        nc.vector.tensor_copy(xb_words[:], table_words[:].bitcast(U32).indirect(two_sb[:]))
         w2_bf = keep.tile([P, PACK * N], BF16, name="w2_bf", tag="rounded", align_bytes=64)
         nc.vector.tensor_copy(dealt(w2_bf, 0, P), w2_raw[:].rearrange("p j (m t) -> p m j t", t=PACK))
         w2_codes = keep.tile([P, N], U32, name="w2_codes", align_bytes=64)
         w2_plane = keep.tile([P, N], U8, name="w2_plane", align_bytes=64)
-        nc.vector.quantize_mx(out=w2_codes[:].bitcast(FP8X4), scales=w2_plane[:], in_=w2_bf[:])
         top_b = keep.tile([P, PACK], F32, name="top_b")
         bias_b = keep.tile([P, PACK], F32, name="bias_b")
         for t in tiles:
+            cols = slice(P * t, P * (t + 1))
+            nc.vector.quantize_mx(
+                out=w2_codes[:, cols].bitcast(FP8X4), scales=w2_plane[:, cols], in_=w2_bf[:, N * t : N * (t + 1)]
+            )
             product(bank_b[t][:], w2_codes, w2_plane, t, xb_words[:], x_planes[:, N:])
+        for t in tiles:
             nc.vector.tensor_scalar(
                 win_b[t][:, :N], bank_b[t][:], 1.0, None, ALU.mult, ALU.max, accum_out=top_b[:, t : t + 1]
             )
@@ -248,27 +252,38 @@ def tile_picked_hkqedfeshega_none_p_kernel(
         out_rows = out.rearrange("(p t) v -> p t v", t=PACK)
         ea4 = logit
         kept = ea_sum
-        win_sq, win_half = win_a, win_b
+        last = PACK - 1
+        win_sq = [win_a[t % 2] for t in tiles]
+        win_half = win_b
+        halves = [(slice(HALF * h, HALF * (h + 1)), slice(HALF // 16 * h, HALF // 16 * (h + 1))) for h in range(2)]
+
+        def square(t):
+            nc.scalar.activation(win_sq[t][:, :N], bank_s[t][:], ACT.Square, scale=0.0625)
+
+        square(0)
+        square(1)
+        for t in (2, 0, 1, 3):
+            nc.vector.tensor_scalar(win_half[t][:, :N], bank_s[t][:], -0.03125, None, ALU.mult)
+        fetched = win_sq[last - 1]
         for t in tiles:
             result = keep.tile([P, N], F32, name="result%d" % t)
-            if t == 0:
-                nc.scalar.activation(win_sq[t][:, :N], bank_s[t][:], ACT.Square, scale=0.0625)
-            if t < PACK - 1:
-                nc.vector.tensor_scalar(win_half[t][:, :N], bank_s[t][:], -0.03125, None, ALU.mult)
-            else:
-                nc.scalar.activation(win_half[t][:, :N], bank_s[t][:], ACT.Copy, scale=-0.03125)
-            if t > 0:
-                nc.scalar.activation(win_sq[t][:, :N], bank_s[t][:], ACT.Square, scale=0.0625)
-            pieces = [(0, N)] if t < PACK - 1 else [(0, HALF), (HALF, N)]
-            for c0, c1 in pieces:
-                entries = slice(c0 // 16, c1 // 16)
-                nc.scalar.activation(
-                    ea4[:, t, c0:c1], win_sq[t][:].indirect(n4_sb[:, entries]), ACT.Exp, scale=neg_tau4[:, t : t + 1]
-                )
+            nc.scalar.activation(
+                ea4[:, t, :], win_sq[t][:].indirect(n4_sb[:]), ACT.Exp, scale=neg_tau4[:, t : t + 1]
+            )
+            if t + 2 <= last:
+                square(t + 2)
+            for cols, entries in halves:
                 nc.vector.scalar_tensor_tensor(
-                    kept[:, t, c0:c1], bank_s[t][:, c0:c1], 0.0625, ea4[:, t, c0:c1], ALU.mult, ALU.mult
+                    kept[:, t, cols], bank_s[t][:, cols], 0.0625, ea4[:, t, cols], ALU.mult, ALU.mult
                 )
-                nc.vector.tensor_tensor(
-                    result[:, c0:c1], win_half[t][:].indirect(n5_sb[:, entries]), kept[:, t, c0:c1], ALU.add
-                )
-                nc.sync.dma_start(out_rows[:, t, c0:c1], result[:, c0:c1])
+            for cols, entries in halves:
+                if t < last:
+                    looked_up = win_half[t][:].indirect(n5_sb[:, entries])
+                else:
+                    nc.scalar.activation(fetched[:, cols], win_half[t][:].indirect(n5_sb[:, entries]), ACT.Copy)
+                    looked_up = fetched[:, cols]
+                nc.vector.tensor_tensor(result[:, cols], looked_up, kept[:, t, cols], ALU.add)
+                if t == last:
+                    nc.sync.dma_start(out_rows[:, t, cols], result[:, cols])
+            if t < last:
+                nc.sync.dma_start(out_rows[:, t, :], result[:])

@@ -21,7 +21,12 @@ PACK = 4
 N = 512
 HALF = N // 2
 WINDOW = 2 * N
-SCALE_ROWS = 16
+GROUP = 16
+QUADRANT = 32
+BLOCKS = K // 32
+COPIES = P // BLOCKS
+HALF_GROUPS = HALF // PACK
+SCALAR_GROUPS = 24
 
 
 def tile_picked_hkqedfeshega_none_p_kernel(
@@ -36,7 +41,7 @@ def tile_picked_hkqedfeshega_none_p_kernel(
         psum = ctx.enter_context(tc.psum_pool(name="psum", bufs=1))
 
         def load_list(name, src):
-            dst = lists.tile([P, N // 16], U16, name=name)
+            dst = lists.tile([P, N // GROUP], U16, name=name)
             nc.sync.dma_start(dst[:], src)
             return dst
 
@@ -45,11 +50,38 @@ def tile_picked_hkqedfeshega_none_p_kernel(
             nc.gpsimd.dma_start(dst[:], src.rearrange("(p t) o -> p (t o)", t=PACK))
             return dst
 
+        def scaled(dst, src, factor):
+            nc.gpsimd.tensor_scalar(dst, src, factor, 0.0, ALU.mult, ALU.add)
+
+        def dealt(grouped, m0, m1):
+            return grouped[:].rearrange("p (t m j) -> p m j t", t=PACK, j=PACK)[:, m0:m1]
+
+        def column_groups(raw):
+            return raw[:].rearrange("p j (m t) -> p m j t", t=PACK)
+
+        def quantize_tile(codes, plane, grouped, t):
+            cols = slice(P * t, P * (t + 1))
+            nc.vector.quantize_mx(
+                out=codes[:, cols].bitcast(FP8X4), scales=plane[:, cols], in_=grouped[:, N * t : N * (t + 1)]
+            )
+
+        def product(bank, lhs_codes, lhs_plane, t, rhs_codes, rhs_plane):
+            cols = slice(P * t, P * (t + 1))
+            nc.tensor.matmul_mx(
+                out=bank,
+                lhsT=lhs_codes[:, cols].bitcast(FP8X4),
+                lhsT_scale=lhs_plane[:, cols],
+                rhs=rhs_codes.bitcast(FP8X4),
+                rhs_scale=rhs_plane,
+                start=True,
+                stop=True,
+            )
+
         offs_sb = load_list("offs_sb", offs)
         table_scales = keep.tile([P, T], U8, name="table_scales", tag="staging")
         nc.scalar.dma_start(
             table_scales[:].bitcast(I32),
-            x_scales[0].bitcast(I32).unsqueeze(1).broadcast_to([SCALE_ROWS, P // SCALE_ROWS, T // 4]),
+            x_scales[0].bitcast(I32).unsqueeze(1).broadcast_to([BLOCKS, COPIES, T // 4]),
         )
         two_sb = load_list("two_sb", two)
         table_words = keep.tile([P, T], I32, name="table_words")
@@ -57,13 +89,9 @@ def tile_picked_hkqedfeshega_none_p_kernel(
         n1_sb = load_list("n1_sb", n1)
         n2_sb = load_list("n2_sb", n2)
         w_raw = [keep.tile([P, PACK, HALF], F32, name="w_raw%d" % h) for h in range(2)]
-
-        def load_weight(w):
-            rows = w.rearrange("(p j) c -> p j c", j=PACK)
-            for h in range(2):
-                nc.sync.dma_start(w_raw[h][:], rows[:, :, h * HALF : (h + 1) * HALF])
-
-        load_weight(w1)
+        w1_rows = w1.rearrange("(p j) c -> p j c", j=PACK)
+        for h in range(2):
+            nc.sync.dma_start(w_raw[h][:], w1_rows[:, :, h * HALF : (h + 1) * HALF])
 
         tau_sb = load_column("tau_sb", tau)
         tau2_sb = load_column("tau2_sb", tau2)
@@ -72,10 +100,6 @@ def tile_picked_hkqedfeshega_none_p_kernel(
         nc.gpsimd.memset(win_a[0][:, N:], 0.0)
         rate_a = keep.tile([P, PACK, 2], F32, name="rate_a")
         neg_tau2 = keep.tile([P, PACK], F32, name="neg_tau2")
-
-        def scaled(dst, src, factor):
-            nc.gpsimd.tensor_scalar(dst, src, factor, 0.0, ALU.mult, ALU.add)
-
         scaled(rate_a[:, :, 0], tau_sb[:], -1.0)
         scaled(rate_a[:, :, 1], tau2_sb[:], 1.0)
         scaled(neg_tau2[:], tau2_sb[:], -1.0)
@@ -99,55 +123,36 @@ def tile_picked_hkqedfeshega_none_p_kernel(
         nc.vector.memset(x_planes[:].bitcast(I32), 0)
         nc.vector.tensor_copy(picked_scales[:, :N], table_scales[:].indirect(offs_sb[:]))
         nc.vector.tensor_copy(picked_scales[:, N:], table_scales[:].indirect(two_sb[:]))
-        for j in range(4):
+        for j in range(QUADRANT // COPIES):
             nc.sync.dma_start(
-                x_planes[:].bitcast(I32)[j:P:32, :], picked_scales[:].bitcast(I32)[8 * j : P : 32, :]
+                x_planes[:].bitcast(I32)[j:P:QUADRANT, :], picked_scales[:].bitcast(I32)[COPIES * j : P : QUADRANT, :]
             )
         w2_raw = keep.tile([P, PACK, N], F32, name="w2_raw", tag="staging")
         nc.sync.dma_start(w2_raw[:], w2.rearrange("(p j) c -> p j c", j=PACK))
         n3_sb = load_list("n3_sb", n3)
         n4_sb = load_list("n4_sb", n4)
         n5_sb = load_list("n5_sb", n5)
-        xa_words = keep.tile([P, N], U32, name="xa_words", tag="picked_words", align_bytes=64)
+        xa_words = keep.tile([P, N], U32, name="xa_words", align_bytes=64)
+        xb_words = keep.tile([P, N], U32, name="xb_words", align_bytes=64)
         nc.vector.tensor_copy(xa_words[:], table_words[:].bitcast(U32).indirect(offs_sb[:]))
-
-        def dealt(grouped, m0, m1):
-            return grouped[:].rearrange("p (t m j) -> p m j t", t=PACK, j=PACK)[:, m0:m1]
-
-        def raw(h, m0, m1):
-            return w_raw[h][:].rearrange("p j (m t) -> p m j t", t=PACK)[:, m0:m1]
+        nc.vector.tensor_copy(xb_words[:], table_words[:].bitcast(U32).indirect(two_sb[:]))
 
         w1_bf = keep.tile([P, PACK * N], BF16, name="w1_bf", align_bytes=64)
-        nc.scalar.activation(dealt(w1_bf, 0, 64), raw(0, 0, 64), ACT.Copy)
-        nc.scalar.activation(dealt(w1_bf, 64, 88), raw(1, 0, 24), ACT.Copy)
-        nc.vector.tensor_copy(dealt(w1_bf, 88, 128), raw(1, 24, 64))
+        split = HALF_GROUPS + SCALAR_GROUPS
+        nc.scalar.activation(dealt(w1_bf, 0, HALF_GROUPS), column_groups(w_raw[0])[:, 0:HALF_GROUPS], ACT.Copy)
+        nc.scalar.activation(dealt(w1_bf, HALF_GROUPS, split), column_groups(w_raw[1])[:, 0:SCALAR_GROUPS], ACT.Copy)
+        nc.vector.tensor_copy(dealt(w1_bf, split, P), column_groups(w_raw[1])[:, SCALAR_GROUPS:HALF_GROUPS])
         w1_codes = keep.tile([P, N], U32, name="w1_codes", align_bytes=64)
         w1_plane = keep.tile([P, N], U8, name="w1_plane", align_bytes=64)
-
         bank_a = [psum.tile([P, N], F32, name="bank_a%d" % t) for t in tiles]
         bank_b = [psum.tile([P, N], F32, name="bank_b%d" % t) for t in tiles]
-
-        def product(bank, lhs_codes, lhs_plane, t, rhs_codes, rhs_plane):
-            cols = slice(P * t, P * (t + 1))
-            nc.tensor.matmul_mx(
-                out=bank,
-                lhsT=lhs_codes[:, cols].bitcast(FP8X4),
-                lhsT_scale=lhs_plane[:, cols],
-                rhs=rhs_codes.bitcast(FP8X4),
-                rhs_scale=rhs_plane,
-                start=True,
-                stop=True,
-            )
-
         for t in tiles:
-            cols = slice(P * t, P * (t + 1))
-            nc.vector.quantize_mx(
-                out=w1_codes[:, cols].bitcast(FP8X4), scales=w1_plane[:, cols], in_=w1_bf[:, N * t : N * (t + 1)]
-            )
+            quantize_tile(w1_codes, w1_plane, w1_bf, t)
             product(bank_a[t][:], w1_codes, w1_plane, t, xa_words[:], x_planes[:, :N])
 
         ends_a = keep.tile([P, PACK, 2], F32, name="ends_a")
         bias_a = keep.tile([P, PACK, 2], F32, name="bias_a")
+        ea = [win_b[t][:, N:] for t in tiles]
         ea2 = keep.tile([P, PACK, N], F32, name="ea2")
         for t in tiles:
             nc.vector.tensor_scalar(
@@ -161,27 +166,21 @@ def tile_picked_hkqedfeshega_none_p_kernel(
             else:
                 nc.vector.tensor_tensor(bias_a[:, t, :], ends_a[:, t, :], rate_a[:, t, :], ALU.mult)
             nc.scalar.activation(
-                win_b[t][:, N:], win_a[t][:].indirect(n1_sb[:]), ACT.Exp,
-                bias=bias_a[:, t, 0:1], scale=tau_sb[:, t : t + 1],
+                ea[t], win_a[t][:].indirect(n1_sb[:]), ACT.Exp, bias=bias_a[:, t, 0:1], scale=tau_sb[:, t : t + 1]
             )
             nc.scalar.activation(
                 ea2[:, t, :], win_a[t][:].indirect(n2_sb[:]), ACT.Exp,
                 bias=bias_a[:, t, 1:2], scale=neg_tau2[:, t : t + 1],
             )
 
-        xb_words = keep.tile([P, N], U32, name="xb_words", tag="picked_words", align_bytes=64)
-        nc.vector.tensor_copy(xb_words[:], table_words[:].bitcast(U32).indirect(two_sb[:]))
         w2_bf = keep.tile([P, PACK * N], BF16, name="w2_bf", tag="rounded", align_bytes=64)
-        nc.vector.tensor_copy(dealt(w2_bf, 0, P), w2_raw[:].rearrange("p j (m t) -> p m j t", t=PACK))
+        nc.vector.tensor_copy(dealt(w2_bf, 0, P), column_groups(w2_raw))
         w2_codes = keep.tile([P, N], U32, name="w2_codes", align_bytes=64)
         w2_plane = keep.tile([P, N], U8, name="w2_plane", align_bytes=64)
         top_b = keep.tile([P, PACK], F32, name="top_b")
         bias_b = keep.tile([P, PACK], F32, name="bias_b")
         for t in tiles:
-            cols = slice(P * t, P * (t + 1))
-            nc.vector.quantize_mx(
-                out=w2_codes[:, cols].bitcast(FP8X4), scales=w2_plane[:, cols], in_=w2_bf[:, N * t : N * (t + 1)]
-            )
+            quantize_tile(w2_codes, w2_plane, w2_bf, t)
             product(bank_b[t][:], w2_codes, w2_plane, t, xb_words[:], x_planes[:, N:])
         for t in tiles:
             nc.vector.tensor_scalar(
@@ -200,7 +199,7 @@ def tile_picked_hkqedfeshega_none_p_kernel(
         ea_sum = keep.tile([P, PACK, N], F32, name="ea_sum")
         z_bf = keep.tile([P, PACK, N], BF16, name="z_bf", tag="rounded", align_bytes=64)
         for t in tiles:
-            nc.gpsimd.tensor_tensor(ea_sum[:, t, :], win_b[t][:, N:], ea2[:, t, :], ALU.add)
+            nc.gpsimd.tensor_tensor(ea_sum[:, t, :], ea[t], ea2[:, t, :], ALU.add)
         for t in tiles:
             nc.vector.scalar_tensor_tensor(
                 z_bf[:, t, :], bank_a[t][:], gain_a[:, t : t + 1], ea_sum[:, t, :], ALU.mult, ALU.mult
@@ -226,11 +225,12 @@ def tile_picked_hkqedfeshega_none_p_kernel(
                     logit[:, t, cols], bank_b[t][:, cols], tau3_sb[:, t : t + 1], rest[:, t, cols], ALU.mult, ALU.subtract
                 )
         nc.vector.quantize_mx(out=z_codes[:].bitcast(FP8X4), scales=z_plane[:], in_=z_grouped[:])
+
         share = ea3
+        bank_s = bank_a
         z2_grouped = keep.tile([P, PACK * N], BF16, name="z2_grouped", align_bytes=64)
         z2_codes = keep.tile([P, N], U32, name="z2_codes", align_bytes=64)
         z2_plane = keep.tile([P, N], U8, name="z2_plane", align_bytes=64)
-        bank_s = bank_a
         for c in range(N // P):
             cols = slice(P * c, P * (c + 1))
             wide = slice(PACK * P * c, PACK * P * (c + 1))
@@ -254,22 +254,28 @@ def tile_picked_hkqedfeshega_none_p_kernel(
         kept = ea_sum
         last = PACK - 1
         win_sq = [win_a[t % 2] for t in tiles]
-        win_half = win_b
-        halves = [(slice(HALF * h, HALF * (h + 1)), slice(HALF // 16 * h, HALF // 16 * (h + 1))) for h in range(2)]
+        win_half = win_b[:last] + [win_sq[last - 1]]
+        halves = [(slice(HALF * h, HALF * (h + 1)), slice(HALF // GROUP * h, HALF // GROUP * (h + 1))) for h in range(2)]
 
         def square(t):
             nc.scalar.activation(win_sq[t][:, :N], bank_s[t][:], ACT.Square, scale=0.0625)
 
         square(0)
         square(1)
-        for t in (2, 0, 1, 3):
+        for t in (2, 0, 1):
             nc.vector.tensor_scalar(win_half[t][:, :N], bank_s[t][:], -0.03125, None, ALU.mult)
-        fetched = win_sq[last - 1]
         for t in tiles:
             result = keep.tile([P, N], F32, name="result%d" % t)
-            nc.scalar.activation(
-                ea4[:, t, :], win_sq[t][:].indirect(n4_sb[:]), ACT.Exp, scale=neg_tau4[:, t : t + 1]
-            )
+            if t < last:
+                nc.scalar.activation(
+                    ea4[:, t, :], win_sq[t][:].indirect(n4_sb[:]), ACT.Exp, scale=neg_tau4[:, t : t + 1]
+                )
+            else:
+                nc.scalar.activation(win_half[t][:, :N], bank_s[t][:], ACT.Copy, scale=-0.03125)
+                for cols, entries in halves:
+                    nc.scalar.activation(
+                        ea4[:, t, cols], win_sq[t][:].indirect(n4_sb[:, entries]), ACT.Exp, scale=neg_tau4[:, t : t + 1]
+                    )
             if t + 2 <= last:
                 square(t + 2)
             for cols, entries in halves:
@@ -277,12 +283,9 @@ def tile_picked_hkqedfeshega_none_p_kernel(
                     kept[:, t, cols], bank_s[t][:, cols], 0.0625, ea4[:, t, cols], ALU.mult, ALU.mult
                 )
             for cols, entries in halves:
-                if t < last:
-                    looked_up = win_half[t][:].indirect(n5_sb[:, entries])
-                else:
-                    nc.scalar.activation(fetched[:, cols], win_half[t][:].indirect(n5_sb[:, entries]), ACT.Copy)
-                    looked_up = fetched[:, cols]
-                nc.vector.tensor_tensor(result[:, cols], looked_up, kept[:, t, cols], ALU.add)
+                nc.vector.tensor_tensor(
+                    result[:, cols], win_half[t][:].indirect(n5_sb[:, entries]), kept[:, t, cols], ALU.add
+                )
                 if t == last:
                     nc.sync.dma_start(out_rows[:, t, cols], result[:, cols])
             if t < last:

from contextlib import ExitStack

import concourse.mybir as mybir

K, T, S, V, H = 512, 2048, 512, 512, 512
FLOPS = 2 * K * H * S + 2 * K * H * V + 2 * H * S * V

F32 = mybir.dt.float32
BF16 = mybir.dt.bfloat16
I32 = mybir.dt.int32
U32 = mybir.dt.uint32
U16 = mybir.dt.uint16
U8 = mybir.dt.uint8
FP8X4 = mybir.dt.float8_e4m3fn_x4
ALU = mybir.AluOpType
ACT = mybir.ActivationFunctionType
AXIS_X = mybir.AxisListType.X

P = 128
PACK = 4
N = 512
HALF = N // 2
WINDOW = 2 * N
GROUP = 16
QUADRANT = 32
BLOCKS = K // 32
COPIES = P // BLOCKS
HALF_GROUPS = HALF // PACK
SCALAR_GROUPS = 24


def tile_picked_hkqedfeshega_none_p_kernel(
    tc, x_words, x_scales, w1, w2, tau, tau2, tau3, ga, gb, tau4, offs, two, n1, n2, n3, n4, n5, out
):
    nc = tc.nc
    tiles = range(PACK)

    with ExitStack() as ctx:
        lists = ctx.enter_context(tc.tile_pool(name="lists", bufs=1))
        keep = ctx.enter_context(tc.tile_pool(name="keep", bufs=1))
        psum = ctx.enter_context(tc.psum_pool(name="psum", bufs=1))

        def load_list(name, src):
            dst = lists.tile([P, N // GROUP], U16, name=name)
            nc.sync.dma_start(dst[:], src)
            return dst

        def load_column(name, src):
            dst = keep.tile([P, PACK], F32, name=name)
            nc.gpsimd.dma_start(dst[:], src.rearrange("(p t) o -> p (t o)", t=PACK))
            return dst

        def scaled(dst, src, factor):
            nc.gpsimd.tensor_scalar(dst, src, factor, 0.0, ALU.mult, ALU.add)

        def dealt(grouped, m0, m1):
            return grouped[:].rearrange("p (t m j) -> p m j t", t=PACK, j=PACK)[:, m0:m1]

        def column_groups(raw):
            return raw[:].rearrange("p j (m t) -> p m j t", t=PACK)

        def quantize_tile(codes, plane, grouped, t):
            cols = slice(P * t, P * (t + 1))
            nc.vector.quantize_mx(
                out=codes[:, cols].bitcast(FP8X4), scales=plane[:, cols], in_=grouped[:, N * t : N * (t + 1)]
            )

        def product(bank, lhs_codes, lhs_plane, t, rhs_codes, rhs_plane):
            cols = slice(P * t, P * (t + 1))
            nc.tensor.matmul_mx(
                out=bank,
                lhsT=lhs_codes[:, cols].bitcast(FP8X4),
                lhsT_scale=lhs_plane[:, cols],
                rhs=rhs_codes.bitcast(FP8X4),
                rhs_scale=rhs_plane,
                start=True,
                stop=True,
            )

        offs_sb = load_list("offs_sb", offs)
        table_scales = keep.tile([P, T], U8, name="table_scales", tag="staging")
        nc.scalar.dma_start(
            table_scales[:].bitcast(I32),
            x_scales[0].bitcast(I32).unsqueeze(1).broadcast_to([BLOCKS, COPIES, T // 4]),
        )
        two_sb = load_list("two_sb", two)
        table_words = keep.tile([P, T], I32, name="table_words")
        nc.sync.dma_start(table_words[:], x_words[0].rearrange("p n t -> p (n t)").bitcast(I32))
        n1_sb = load_list("n1_sb", n1)
        n2_sb = load_list("n2_sb", n2)
        w_raw = [keep.tile([P, PACK, HALF], F32, name="w_raw%d" % h) for h in range(2)]
        w1_rows = w1.rearrange("(p j) c -> p j c", j=PACK)
        for h in range(2):
            nc.sync.dma_start(w_raw[h][:], w1_rows[:, :, h * HALF : (h + 1) * HALF])

        tau_sb = load_column("tau_sb", tau)
        tau2_sb = load_column("tau2_sb", tau2)
        win_a = [keep.tile([P, WINDOW], F32, name="win_a%d" % t) for t in tiles]
        win_b = [keep.tile([P, WINDOW], F32, name="win_b%d" % t) for t in tiles]
        nc.gpsimd.memset(win_a[0][:, N:], 0.0)
        rate_a = keep.tile([P, PACK, 2], F32, name="rate_a")
        neg_tau2 = keep.tile([P, PACK], F32, name="neg_tau2")
        scaled(rate_a[:, :, 0], tau_sb[:], -1.0)
        scaled(rate_a[:, :, 1], tau2_sb[:], 1.0)
        scaled(neg_tau2[:], tau2_sb[:], -1.0)
        for t in tiles[1:]:
            nc.gpsimd.memset(win_a[t][:, N:], 0.0)
        ga_sb = load_column("ga_sb", ga)
        tau3_sb = load_column("tau3_sb", tau3)
        gb_sb = load_column("gb_sb", gb)
        tau4_sb = load_column("tau4_sb", tau4)
        gain_a = keep.tile([P, PACK], F32, name="gain_a")
        gain_b = keep.tile([P, PACK], F32, name="gain_b")
        neg_tau4 = keep.tile([P, PACK], F32, name="neg_tau4")
        quarter = keep.tile([P, 1], F32, name="quarter")
        scaled(gain_a[:], ga_sb[:], 1.5)
        scaled(gain_b[:], gb_sb[:], 2.0)
        scaled(neg_tau4[:], tau4_sb[:], -1.0)
        nc.gpsimd.memset(quarter[:], 0.25)

        picked_scales = keep.tile([P, 2 * N], U8, name="picked_scales")
        x_planes = keep.tile([P, 2 * N], U8, name="x_planes", align_bytes=64)
        nc.vector.memset(x_planes[:].bitcast(I32), 0)
        nc.vector.tensor_copy(picked_scales[:, :N], table_scales[:].indirect(offs_sb[:]))
        nc.vector.tensor_copy(picked_scales[:, N:], table_scales[:].indirect(two_sb[:]))
        for j in range(QUADRANT // COPIES):
            nc.sync.dma_start(
                x_planes[:].bitcast(I32)[j:P:QUADRANT, :], picked_scales[:].bitcast(I32)[COPIES * j : P : QUADRANT, :]
            )
        w2_raw = keep.tile([P, PACK, N], F32, name="w2_raw", tag="staging")
        nc.sync.dma_start(w2_raw[:], w2.rearrange("(p j) c -> p j c", j=PACK))
        n3_sb = load_list("n3_sb", n3)
        n4_sb = load_list("n4_sb", n4)
        n5_sb = load_list("n5_sb", n5)
        xa_words = keep.tile([P, N], U32, name="xa_words", align_bytes=64)
        xb_words = keep.tile([P, N], U32, name="xb_words", align_bytes=64)
        nc.vector.tensor_copy(xa_words[:], table_words[:].bitcast(U32).indirect(offs_sb[:]))
        nc.vector.tensor_copy(xb_words[:], table_words[:].bitcast(U32).indirect(two_sb[:]))

        w1_bf = keep.tile([P, PACK * N], BF16, name="w1_bf", align_bytes=64)
        split = HALF_GROUPS + SCALAR_GROUPS
        nc.scalar.activation(dealt(w1_bf, 0, HALF_GROUPS), column_groups(w_raw[0])[:, 0:HALF_GROUPS], ACT.Copy)
        nc.scalar.activation(dealt(w1_bf, HALF_GROUPS, split), column_groups(w_raw[1])[:, 0:SCALAR_GROUPS], ACT.Copy)
        nc.vector.tensor_copy(dealt(w1_bf, split, P), column_groups(w_raw[1])[:, SCALAR_GROUPS:HALF_GROUPS])
        w1_codes = keep.tile([P, N], U32, name="w1_codes", align_bytes=64)
        w1_plane = keep.tile([P, N], U8, name="w1_plane", align_bytes=64)
        bank_a = [psum.tile([P, N], F32, name="bank_a%d" % t) for t in tiles]
        bank_b = [psum.tile([P, N], F32, name="bank_b%d" % t) for t in tiles]
        for t in tiles:
            quantize_tile(w1_codes, w1_plane, w1_bf, t)
            product(bank_a[t][:], w1_codes, w1_plane, t, xa_words[:], x_planes[:, :N])

        ends_a = keep.tile([P, PACK, 2], F32, name="ends_a")
        bias_a = keep.tile([P, PACK, 2], F32, name="bias_a")
        ea = [win_b[t][:, N:] for t in tiles]
        ea2 = keep.tile([P, PACK, N], F32, name="ea2")
        for t in tiles:
            nc.vector.tensor_scalar(
                win_a[t][:, :N], bank_a[t][:], 1.0, None, ALU.mult, ALU.max, accum_out=ends_a[:, t, 0:1]
            )
            if t == 0:
                nc.vector.tensor_tensor(bias_a[:, t, 0:1], ends_a[:, t, 0:1], rate_a[:, t, 0:1], ALU.mult)
            nc.vector.tensor_reduce(ends_a[:, t, 1:2], bank_a[t][:], AXIS_X, ALU.min)
            if t == 0:
                nc.vector.tensor_tensor(bias_a[:, t, 1:2], ends_a[:, t, 1:2], rate_a[:, t, 1:2], ALU.mult)
            else:
                nc.vector.tensor_tensor(bias_a[:, t, :], ends_a[:, t, :], rate_a[:, t, :], ALU.mult)
            nc.scalar.activation(
                ea[t], win_a[t][:].indirect(n1_sb[:]), ACT.Exp, bias=bias_a[:, t, 0:1], scale=tau_sb[:, t : t + 1]
            )
            nc.scalar.activation(
                ea2[:, t, :], win_a[t][:].indirect(n2_sb[:]), ACT.Exp,
                bias=bias_a[:, t, 1:2], scale=neg_tau2[:, t : t + 1],
            )

        w2_bf = keep.tile([P, PACK * N], BF16, name="w2_bf", tag="rounded", align_bytes=64)
        nc.vector.tensor_copy(dealt(w2_bf, 0, P), column_groups(w2_raw))
        w2_codes = keep.tile([P, N], U32, name="w2_codes", align_bytes=64)
        w2_plane = keep.tile([P, N], U8, name="w2_plane", align_bytes=64)
        top_b = keep.tile([P, PACK], F32, name="top_b")
        bias_b = keep.tile([P, PACK], F32, name="bias_b")
        for t in tiles:
            quantize_tile(w2_codes, w2_plane, w2_bf, t)
            product(bank_b[t][:], w2_codes, w2_plane, t, xb_words[:], x_planes[:, N:])
        for t in tiles:
            nc.vector.tensor_scalar(
                win_b[t][:, :N], bank_b[t][:], 1.0, None, ALU.mult, ALU.max, accum_out=top_b[:, t : t + 1]
            )
            nc.vector.tensor_scalar(
                bias_b[:, t : t + 1], top_b[:, t : t + 1], tau3_sb[:, t : t + 1], -1.0, ALU.mult, ALU.mult
            )
        ea3 = keep.tile([P, PACK, N], F32, name="ea3")
        for t in tiles:
            nc.scalar.activation(
                ea3[:, t, :], win_b[t][:].indirect(n3_sb[:]), ACT.Exp,
                bias=bias_b[:, t : t + 1], scale=tau3_sb[:, t : t + 1],
            )

        ea_sum = keep.tile([P, PACK, N], F32, name="ea_sum")
        z_bf = keep.tile([P, PACK, N], BF16, name="z_bf", tag="rounded", align_bytes=64)
        for t in tiles:
            nc.gpsimd.tensor_tensor(ea_sum[:, t, :], ea[t], ea2[:, t, :], ALU.add)
        for t in tiles:
            nc.vector.scalar_tensor_tensor(
                z_bf[:, t, :], bank_a[t][:], gain_a[:, t : t + 1], ea_sum[:, t, :], ALU.mult, ALU.mult
            )
        z_grouped = keep.tile([P, PACK * N], BF16, name="z_grouped", align_bytes=64)
        nc.vector.tensor_copy(
            z_grouped[:].rearrange("p (u m t) -> p m t u", u=PACK, t=PACK),
            z_bf[:].rearrange("p t (m u) -> p m t u", u=PACK),
        )
        z_codes = keep.tile([P, N], U32, name="z_codes", align_bytes=64)
        z_plane = keep.tile([P, N], U8, name="z_plane", align_bytes=64)

        b_gain = keep.tile([P, PACK, N], F32, name="b_gain")
        for t in tiles:
            nc.gpsimd.tensor_scalar(b_gain[:, t, :], win_b[t][:, :N], gain_b[:, t : t + 1], 0.0, ALU.mult, ALU.add)
        rest = keep.tile([P, PACK, N], F32, name="rest")
        logit = keep.tile([P, PACK, N], F32, name="logit")
        for h in range(2):
            cols = slice(HALF * h, HALF * (h + 1))
            nc.scalar.activation(rest[:, :, cols], ea3[:, :, cols], ACT.Ln, bias=quarter[:])
            for t in tiles:
                nc.vector.scalar_tensor_tensor(
                    logit[:, t, cols], bank_b[t][:, cols], tau3_sb[:, t : t + 1], rest[:, t, cols], ALU.mult, ALU.subtract
                )
        nc.vector.quantize_mx(out=z_codes[:].bitcast(FP8X4), scales=z_plane[:], in_=z_grouped[:])

        share = ea3
        bank_s = bank_a
        z2_grouped = keep.tile([P, PACK * N], BF16, name="z2_grouped", align_bytes=64)
        z2_codes = keep.tile([P, N], U32, name="z2_codes", align_bytes=64)
        z2_plane = keep.tile([P, N], U8, name="z2_plane", align_bytes=64)
        for c in range(N // P):
            cols = slice(P * c, P * (c + 1))
            wide = slice(PACK * P * c, PACK * P * (c + 1))
            for t in tiles:
                nc.scalar.activation(share[:, t, cols], logit[:, t, cols], ACT.Sigmoid, bias=bias_b[:, t : t + 1])
            nc.vector.tensor_tensor(
                z2_grouped[:, wide].rearrange("p (c i t) -> p c t i", i=2, t=PACK),
                b_gain[:, :, cols].rearrange("p t (c i) -> p c t i", i=2),
                share[:, :, cols].rearrange("p t (c i) -> p c t i", i=2),
                ALU.mult,
            )
            nc.vector.quantize_mx(out=z2_codes[:, cols].bitcast(FP8X4), scales=z2_plane[:, cols], in_=z2_grouped[:, wide])
            for t in tiles:
                product(bank_s[t][:, cols], z_codes, z_plane, t, z2_codes[:, cols], z2_plane[:, cols])

        table_warm = keep.tile([P, 1], F32, name="table_warm")
        nc.scalar.activation(table_warm[:], share[:, 0, N - 1 : N], ACT.Exp)

        out_rows = out.rearrange("(p t) v -> p t v", t=PACK)
        ea4 = logit
        kept = ea_sum
        last = PACK - 1
        win_sq = [win_a[t % 2] for t in tiles]
        win_half = win_b[:last] + [win_sq[last - 1]]
        halves = [(slice(HALF * h, HALF * (h + 1)), slice(HALF // GROUP * h, HALF // GROUP * (h + 1))) for h in range(2)]

        def square(t):
            nc.scalar.activation(win_sq[t][:, :N], bank_s[t][:], ACT.Square, scale=0.0625)

        square(0)
        square(1)
        for t in (2, 0, 1):
            nc.vector.tensor_scalar(win_half[t][:, :N], bank_s[t][:], -0.03125, None, ALU.mult)
        for t in tiles:
            result = keep.tile([P, N], F32, name="result%d" % t)
            if t < last:
                nc.scalar.activation(
                    ea4[:, t, :], win_sq[t][:].indirect(n4_sb[:]), ACT.Exp, scale=neg_tau4[:, t : t + 1]
                )
            else:
                nc.scalar.activation(win_half[t][:, :N], bank_s[t][:], ACT.Copy, scale=-0.03125)
                for cols, entries in halves:
                    nc.scalar.activation(
                        ea4[:, t, cols], win_sq[t][:].indirect(n4_sb[:, entries]), ACT.Exp, scale=neg_tau4[:, t : t + 1]
                    )
            if t + 2 <= last:
                square(t + 2)
            for cols, entries in halves:
                nc.vector.scalar_tensor_tensor(
                    kept[:, t, cols], bank_s[t][:, cols], 0.0625, ea4[:, t, cols], ALU.mult, ALU.mult
                )
            for cols, entries in halves:
                nc.vector.tensor_tensor(
                    result[:, cols], win_half[t][:].indirect(n5_sb[:, entries]), kept[:, t, cols], ALU.add
                )
                if t == last:
                    nc.sync.dma_start(out_rows[:, t, cols], result[:, cols])
            if t < last:
                nc.sync.dma_start(out_rows[:, t, :], result[:])
